import numpy as np
import ml_dtypes


def mxq(x, axis, fmt="e4m3"):
    dtype, down = {"e4m3": (ml_dtypes.float8_e4m3fn, 7), "e5m2": (ml_dtypes.float8_e5m2, 14)}[fmt]
    v = np.moveaxis(np.asarray(x, np.float32).astype(ml_dtypes.bfloat16).astype(np.float64), axis, -1)
    blocks = v.reshape(v.shape[:-1] + (-1, 32))
    amax = np.abs(blocks).max(-1, keepdims=True)
    byte = np.maximum(np.where(amax > 0, np.frexp(amax)[1] - 1 + 127, 0) - down, 1)
    scale = np.exp2(byte - 127.0)
    codes = (blocks / scale).astype(np.float32).astype(dtype).astype(np.float64)
    return np.moveaxis((codes * scale).reshape(v.shape), -1, axis)


WIDE = False


def mx_kscale(k):
    if not WIDE:
        return np.ones(k)
    levels = np.array([10, -10, 5, -5, 0])
    if k % 512:
        return np.exp2(np.random.permutation(np.resize(levels, k // 32))).repeat(32)
    a = np.empty((k // 512, 16))
    for p in range(k // 512):
        a[p, :8] = np.random.permutation(np.resize(levels, 8))
        for g in range(8):
            far = levels[np.abs(levels - a[p, g]) >= 10]
            a[p, g + 8] = far[np.random.randint(len(far))]
    return np.exp2(a.ravel()).repeat(32)


def f64(x):
    return np.asarray(x).astype(np.float64)


def striped(idx):
    return np.tile(np.asarray(idx).reshape(-1, 16).T, (8, 1)).astype(np.uint16)


def unstriped(offs):
    return offs[:16].T.reshape(-1).astype(np.int64)


def striped8(idx):
    return np.asarray(idx).reshape(8, -1, 16).transpose(0, 2, 1).reshape(128, -1).astype(np.uint16)


def unstriped8(offs):
    return offs.reshape(8, 16, -1).transpose(0, 2, 1).reshape(8, -1).astype(np.int64)


def pick8(x, idx, run):
    r = np.arange(len(x))
    return x[r[:, None], idx[r % (8 * run) // run]]


E2M1 = np.array([0.0, 0.5, 1.0, 1.5, 2.0, 3.0, 4.0, 6.0, -0.0, -0.5, -1.0, -1.5, -2.0, -3.0, -4.0, -6.0])


def pack_weight(w, fmt):
    k, n = w.shape
    w = f64(np.asarray(w, np.float32).astype(ml_dtypes.bfloat16)).reshape(k // 32, 32, n)
    amax = np.abs(w).max(1)
    if fmt == "e4m3":
        byte = np.frexp(amax)[1] - 1 + 127 - 7
    else:
        mant, ex = np.frexp(amax / 6.0)
        byte = np.where(mant > 0.5, ex, ex - 1) + 127
    byte = np.clip(np.where(amax > 0, byte, 1), 1, 254)
    scaled = (w * np.exp2(127.0 - byte)[:, None, :]).reshape(k, n).astype(np.float32)
    by_word = np.ascontiguousarray(scaled.reshape(k // 512, 128, 4, n).transpose(0, 1, 3, 2))
    if fmt == "e4m3":
        words = by_word.astype(ml_dtypes.float8_e4m3fn).view(np.uint8)
    else:
        c = by_word.astype(ml_dtypes.float4_e2m1fn).view(np.uint8) & 0xF
        words = (c[..., 0::2] | (c[..., 1::2] << 4)).reshape(k // 512, 128, 2 * n)
    return np.ascontiguousarray(words), np.ascontiguousarray(byte.astype(np.uint8).reshape(k // 512, 16, n))


def unpack_weight(words, scales, fmt):
    g, _, n = scales.shape
    words = np.ascontiguousarray(words).reshape(g, 128, n, -1)
    if fmt == "e4m3":
        vals = words.view(ml_dtypes.float8_e4m3fn).astype(np.float64)
    else:
        nib = np.empty((g, 128, n, 4), np.uint8)
        nib[..., 0::2] = words & 0xF
        nib[..., 1::2] = words >> 4
        vals = E2M1[nib]
    vals = vals * np.repeat(np.exp2(scales.astype(np.float64) - 127.0), 8, axis=1)[..., None]
    return vals.transpose(0, 1, 3, 2).reshape(g * 512, n)


K, J, R, T, U, F, C, O, N, S = 512, 512, 512, 2048, 1024, 1024, 1024, 256, 256, 1024


def setup_inputs():
    n = np.random.standard_normal
    idx = np.stack([np.random.permutation(T)[:U] for _ in range(8)])
    idx2 = np.random.permutation(U)[:J]
    idx3 = np.random.permutation(F)[:R]
    idx4 = np.random.permutation(C)[:J]
    idx5 = np.random.permutation(C)[:O]
    idx6 = np.stack([np.random.permutation(C)[:O] for _ in range(8)])
    idx7 = np.random.permutation(S)[:N]
    fk = mx_kscale(K)
    fr = mx_kscale(R)
    tr = np.ones(F)
    tr[idx3] = fr
    wtp = pack_weight(n((K, F)) * 1 / np.sqrt(K) / fk[:, None] * tr, "e2m1")
    vsp = pack_weight(n((R, S)) * 1 / np.sqrt(R) / fr[:, None], "e4m3")
    return {
        "ta": (np.random.randint(-7, 8, (K, T)).astype(np.float64)).astype(np.float32),
        "ga": ((np.random.randint(8, 25, (K, 1)) / 64.0) * fk[:, None]).astype(np.float32),
        "gb": (np.random.uniform(0.5, 1.6, (K, 1))).astype(np.float32),
        "wt_words": wtp[0],
        "wt_scales": wtp[1],
        "sa": (np.random.uniform(0.5, 1.6, (R, 1))).astype(np.float32),
        "sb": (np.random.uniform(0.5, 1.6, (R, 1))).astype(np.float32),
        "vs_words": vsp[0],
        "vs_scales": vsp[1],
        "offs": striped8(idx),
        "offs2": striped(idx2),
        "offs3": striped(idx3),
        "offs4": striped(idx4),
        "offs5": striped(idx5),
        "offs6": striped8(idx6),
        "offs7": striped(idx7),
    }


def reference(ta, ga, gb, wt_words, wt_scales, sa, sb, vs_words, vs_scales, offs, offs2, offs3, offs4, offs5, offs6, offs7):
    idx = unstriped8(offs)
    idx2 = unstriped(offs2)
    idx3 = unstriped(offs3)
    idx4 = unstriped(offs4)
    idx5 = unstriped(offs5)
    idx6 = unstriped8(offs6)
    idx7 = unstriped(offs7)
    wtu = unpack_weight(wt_words, wt_scales, "e2m1")
    vsu = unpack_weight(vs_words, vs_scales, "e4m3")
    xcd = pick8(f64(ta), idx, 64) * f64(ga)
    xc = xcd[:, idx2] * f64(gb)
    wtidx3g = wtu[:, idx3]
    xcq = mxq(xc, 0, "e4m3")
    a = wtidx3g.T @ xcq
    pw = np.zeros((R, C))
    pw[:, idx4] = a
    hid = np.abs(pw[:, idx5] * f64(sa) - pick8(pw, idx6, 64) * f64(sb))
    vsidx7g = vsu[:, idx7]
    hidq = mxq(hid, 0, "e4m3")
    y = vsidx7g.T @ hidq
    return y

@@ -1,0 +1,210 @@
+from contextlib import ExitStack
+
+import concourse.mybir as mybir
+
+K, J, R, T, U, F, C, O, N, S = 512, 512, 512, 2048, 1024, 1024, 1024, 256, 256, 1024
+FLOPS = 2 * K * R * J + 2 * R * N * O
+
+F32 = mybir.dt.float32
+BF16 = mybir.dt.bfloat16
+I32 = mybir.dt.int32
+U32 = mybir.dt.uint32
+U16 = mybir.dt.uint16
+U8 = mybir.dt.uint8
+FP8X4 = mybir.dt.float8_e4m3fn_x4
+FP4X4 = mybir.dt.float4_e2m1fn_x4
+ACT = mybir.ActivationFunctionType
+ALU = mybir.AluOpType
+
+P = 128
+PACK = 4
+HALF = J // 2
+STRIPE = 16
+ALIGN = 64
+
+
+def tile_picked_respelled_store_one_boardmixed_store_plain_kernel(
+    tc, ta, ga, gb, wt_words, wt_scales, sa, sb, vs_words, vs_scales,
+    offs, offs2, offs3, offs4, offs5, offs6, offs7, out,
+):
+    nc = tc.nc
+    with ExitStack() as ctx:
+        keep = ctx.enter_context(tc.tile_pool(name="keep", bufs=1))
+        psum = ctx.enter_context(tc.psum_pool(name="psum", bufs=1))
+
+        def new(name, shape, dtype, tag=None):
+            return keep.tile(shape, dtype, name=name, tag=tag or name, align_bytes=ALIGN)
+
+        def load_list(name, source):
+            tile = new(name, list(source.shape), U16)
+            nc.sync.dma_start(tile[:], source)
+            return tile
+
+        def load_column(name, source, queue):
+            tile = new(name, [P, PACK], F32)
+            queue.dma_start(tile[:], source.rearrange("(p t) o -> p (t o)", t=PACK))
+            return tile
+
+        def load_scale_rows(name, source, width):
+            staged = new(name + "_staged", [PACK, PACK, width // 4], I32)
+            nc.scalar.dma_start(staged[:], source[0].bitcast(I32).rearrange("(q i) c -> i q c", i=PACK))
+            plane = new(name + "_plane", [P, width], U8)
+            nc.vector.memset(plane[:].bitcast(I32), 0)
+            for q in range(4):
+                nc.vector.tensor_copy(plane[32 * q : 32 * q + PACK, :].bitcast(I32), staged[:, q, :])
+            return plane
+
+        ta_rows = ta.rearrange("(p t) c -> t p c", t=PACK)
+        ta_sb = [new("ta%d" % t, [P, T], F32) for t in range(PACK)]
+
+        ga_sb = load_column("ga", ga, nc.scalar)
+        gb_sb = load_column("gb", gb, nc.scalar)
+        offs_sb = load_list("offs", offs)
+        nc.sync.dma_start(ta_sb[0][:], ta_rows[0])
+        offs2_sb = load_list("offs2", offs2)
+        nc.sync.dma_start(ta_sb[1][:], ta_rows[1])
+        nc.sync.dma_start(ta_sb[2][:], ta_rows[2])
+        wt_words_sb = new("wt_words", [P, 2 * F], U8)
+        nc.sync.dma_start(wt_words_sb[:].bitcast(I32), wt_words[0].bitcast(I32))
+        offs3_sb = load_list("offs3", offs3)
+        nc.sync.dma_start(ta_sb[3][:], ta_rows[3])
+        vs_words_sb = new("vs_words", [P, S], I32)
+        nc.sync.dma_start(vs_words_sb[:], vs_words[0].rearrange("p n t -> p (n t)").bitcast(I32))
+        offs4_sb = load_list("offs4", offs4)
+        offs7_sb = load_list("offs7", offs7)
+        offs5_sb = load_list("offs5", offs5)
+        offs6_sb = load_list("offs6", offs6)
+
+        wt_plane = load_scale_rows("wt_scales", wt_scales, F)
+        vs_plane = load_scale_rows("vs_scales", vs_scales, S)
+        sa_sb = load_column("sa", sa, nc.scalar)
+        sb_sb = load_column("sb", sb, nc.scalar)
+
+        board = [new("board%d" % t, [P, C], F32) for t in range(PACK)]
+        for t in range(PACK):
+            nc.vector.memset(board[t][:], 0.0)
+
+        wt_picked_scales = new("wt_picked_scales", [P, R], U8)
+        nc.vector.tensor_copy(wt_picked_scales[:], wt_plane[:].indirect(offs3_sb[:]))
+        wt_picked_words = new("wt_picked_words", [P, 2 * R], U8)
+        nc.vector.tensor_copy(wt_picked_words[:].bitcast(U16), wt_words_sb[:].bitcast(U16).indirect(offs3_sb[:]))
+        wt_dealt_scales = new("wt_dealt_scales", [P, R], U8)
+        nc.vector.tensor_copy(
+            wt_dealt_scales[:].rearrange("p (t m) -> p t m", t=PACK),
+            wt_picked_scales[:].rearrange("p (m t) -> p t m", t=PACK),
+        )
+        wt_dealt_words = new("wt_dealt_words", [P, 2 * R], U8)
+        nc.vector.tensor_copy(
+            wt_dealt_words[:].rearrange("p (t m b) -> p t m b", t=PACK, b=2),
+            wt_picked_words[:].rearrange("p (m t b) -> p t m b", t=PACK, b=2),
+        )
+        vs_picked_scales = new("vs_picked_scales", [P, N], U8)
+        nc.vector.tensor_copy(vs_picked_scales[:], vs_plane[:].indirect(offs7_sb[:]))
+        vs_picked_words = new("vs_picked_words", [P, N], U32)
+        nc.vector.tensor_copy(vs_picked_words[:], vs_words_sb[:].bitcast(U32).indirect(offs7_sb[:]))
+
+        xcd = [new("xcd%d" % t, [P, U], F32) for t in range(PACK)]
+
+        def half_of(offsets, h):
+            cols = HALF // STRIPE
+            return offsets[:, h * cols : (h + 1) * cols]
+
+        def read_slots(planes, t, h):
+            nc.scalar.activation(
+                planes[:, t, :], xcd[t][:].indirect(half_of(offs2_sb, h)), ACT.Copy, scale=gb_sb[:, t : t + 1]
+            )
+
+        def quantize_slots(planes, h, woven_tag, codes_tag):
+            woven = new("xc_woven%d" % h, [P, HALF, PACK], BF16, woven_tag)
+            nc.vector.tensor_copy(woven[:], planes[:].rearrange("p t j -> p j t"))
+            codes = new("xc_codes%d" % h, [P, HALF], U32, codes_tag)
+            scales = new("xc_scales%d" % h, [P, HALF], U8)
+            nc.vector.quantize_mx(codes[:].bitcast(FP8X4), scales[:], woven[:].rearrange("p j t -> p (j t)"))
+            return codes, scales
+
+        def first_product(quantized, h, pair):
+            codes, scales = quantized
+            acc = psum.tile([P, 2, HALF], F32, name="acc%d%d" % (h, pair[0]))
+            for i, t in enumerate(pair):
+                nc.tensor.matmul_mx(
+                    out=acc[:, i, :],
+                    lhsT=wt_dealt_words[:, 2 * P * t : 2 * P * (t + 1)].bitcast(FP4X4),
+                    lhsT_scale=wt_dealt_scales[:, P * t : P * (t + 1)],
+                    rhs=codes[:].bitcast(FP8X4),
+                    rhs_scale=scales[:],
+                    start=True,
+                    stop=True,
+                )
+            return acc
+
+        def copy_out(engine, acc, h, pair, tag=None):
+            a = new("a%d%d" % (h, pair[0]), [P, 2, HALF], F32, tag)
+            if engine == "vector":
+                nc.vector.tensor_copy(a[:], acc[:])
+            else:
+                nc.scalar.activation(a[:], acc[:], ACT.Copy)
+            return {t: a[:, i, :] for i, t in enumerate(pair)}
+
+        def scatter(engine, a, h, t):
+            window = board[t][:].indirect(half_of(offs4_sb, h))
+            if engine == "vector":
+                nc.vector.tensor_copy(window, a[t])
+            else:
+                nc.scalar.activation(window, a[t], ACT.Copy)
+
+        planes0 = new("xc_planes0", [P, PACK, HALF], BF16)
+        for t in range(PACK):
+            nc.scalar.activation(xcd[t][:], ta_sb[t][:].indirect(offs_sb[:]), ACT.Copy, scale=ga_sb[:, t : t + 1])
+            read_slots(planes0, t, 0)
+        planes1 = new("xc_planes1", [P, PACK, HALF], BF16, "ta3")
+        for t in range(PACK):
+            read_slots(planes1, t, 1)
+
+        xq0 = quantize_slots(planes0, 0, None, "turn")
+        acc_32 = first_product(xq0, 0, (3, 2))
+        acc_01 = first_product(xq0, 0, (0, 1))
+        a0 = copy_out("vector", acc_32, 0, (3, 2))
+        xq1 = quantize_slots(planes1, 1, "turn", None)
+        a0 = {**a0, **copy_out("vector", acc_01, 0, (0, 1), "turn")}
+        scatter("scalar", a0, 0, 3)
+        scatter("scalar", a0, 0, 2)
+        scatter("vector", a0, 0, 0)
+        scatter("vector", a0, 0, 1)
+        a1 = copy_out("scalar", first_product(xq1, 1, (3, 0)), 1, (3, 0))
+        a1 = {**a1, **copy_out("scalar", first_product(xq1, 1, (1, 2)), 1, (1, 2))}
+        scatter("scalar", a1, 1, 3)
+        for t in (0, 1, 2):
+            scatter("vector", a1, 1, t)
+
+        diff = new("diff", [P, PACK, O], F32)
+        for t in (3, 0, 1, 2):
+            first = new("first%d" % t, [P, O], F32)
+            nc.scalar.activation(first[:], board[t][:].indirect(offs5_sb[:]), ACT.Copy, scale=sa_sb[:, t : t + 1])
+            second = new("second%d" % t, [P, O], F32)
+            nc.scalar.activation(second[:], board[t][:].indirect(offs6_sb[:]), ACT.Copy, scale=sb_sb[:, t : t + 1])
+            nc.vector.tensor_tensor(diff[:, t, :], first[:], second[:], ALU.subtract)
+
+        hid = new("hid", [P, O, PACK], BF16)
+        nc.scalar.activation(hid[:], diff[:].rearrange("p t o -> p o t"), ACT.Abs)
+        hid_codes = new("hid_codes", [P, O], U32)
+        hid_scales = new("hid_scales", [P, O], U8)
+        nc.vector.quantize_mx(hid_codes[:].bitcast(FP8X4), hid_scales[:], hid[:].rearrange("p o t -> p (o t)"))
+
+        for i in range(N // P):
+            y = psum.tile([P, O], F32, name="y%d" % i)
+            nc.tensor.matmul_mx(
+                out=y[:],
+                lhsT=vs_picked_words[:, P * i : P * (i + 1)].bitcast(FP8X4),
+                lhsT_scale=vs_picked_scales[:, P * i : P * (i + 1)],
+                rhs=hid_codes[:].bitcast(FP8X4),
+                rhs_scale=hid_scales[:],
+                start=True,
+                stop=True,
+            )
+            y_sb = new("y_sb%d" % i, [P, O], F32)
+            if i == 0:
+                nc.vector.tensor_copy(y_sb[:], y[:])
+                nc.sync.dma_start(out[P * i : P * (i + 1), :], y_sb[:])
+            else:
+                nc.scalar.activation(y_sb[:], y[:], ACT.Copy)
+                nc.scalar.dma_start(out[P * i : P * (i + 1), :], y_sb[:])

@@ -21,6 +21,8 @@ PACK = 4
 HALF = J // 2
 STRIPE = 16
 ALIGN = 64
+RUN = 4
+SPLIT = 160
 
 
 def tile_picked_respelled_store_one_boardmixed_store_plain_kernel(
@@ -47,7 +49,7 @@ def tile_picked_respelled_store_one_boardmixed_store_plain_kernel(
 
         def load_scale_rows(name, source, width):
             staged = new(name + "_staged", [PACK, PACK, width // 4], I32)
-            nc.scalar.dma_start(staged[:], source[0].bitcast(I32).rearrange("(q i) c -> i q c", i=PACK))
+            nc.sync.dma_start(staged[:], source[0].bitcast(I32).rearrange("(q i) c -> i q c", i=PACK))
             plane = new(name + "_plane", [P, width], U8)
             nc.vector.memset(plane[:].bitcast(I32), 0)
             for q in range(4):
@@ -57,28 +59,31 @@ def tile_picked_respelled_store_one_boardmixed_store_plain_kernel(
         ta_rows = ta.rearrange("(p t) c -> t p c", t=PACK)
         ta_sb = [new("ta%d" % t, [P, T], F32) for t in range(PACK)]
 
+        warm = new("warm", [P, 1], F32)
+        nc.vector.memset(warm[:], 0.0)
+        warm_out = new("warm_out", [P, 1], F32)
+        nc.scalar.activation(warm_out[:], warm[:], ACT.Copy)
         ga_sb = load_column("ga", ga, nc.scalar)
-        gb_sb = load_column("gb", gb, nc.scalar)
         offs_sb = load_list("offs", offs)
         nc.sync.dma_start(ta_sb[0][:], ta_rows[0])
+        gb_sb = load_column("gb", gb, nc.sync)
         offs2_sb = load_list("offs2", offs2)
         nc.sync.dma_start(ta_sb[1][:], ta_rows[1])
         nc.sync.dma_start(ta_sb[2][:], ta_rows[2])
+        wt_plane = load_scale_rows("wt_scales", wt_scales, F)
         wt_words_sb = new("wt_words", [P, 2 * F], U8)
         nc.sync.dma_start(wt_words_sb[:].bitcast(I32), wt_words[0].bitcast(I32))
         offs3_sb = load_list("offs3", offs3)
         nc.sync.dma_start(ta_sb[3][:], ta_rows[3])
+        offs4_sb = load_list("offs4", offs4)
+        vs_plane = load_scale_rows("vs_scales", vs_scales, S)
         vs_words_sb = new("vs_words", [P, S], I32)
         nc.sync.dma_start(vs_words_sb[:], vs_words[0].rearrange("p n t -> p (n t)").bitcast(I32))
-        offs4_sb = load_list("offs4", offs4)
         offs7_sb = load_list("offs7", offs7)
         offs5_sb = load_list("offs5", offs5)
         offs6_sb = load_list("offs6", offs6)
-
-        wt_plane = load_scale_rows("wt_scales", wt_scales, F)
-        vs_plane = load_scale_rows("vs_scales", vs_scales, S)
-        sa_sb = load_column("sa", sa, nc.scalar)
-        sb_sb = load_column("sb", sb, nc.scalar)
+        sa_sb = load_column("sa", sa, nc.sync)
+        sb_sb = load_column("sb", sb, nc.sync)
 
         board = [new("board%d" % t, [P, C], F32) for t in range(PACK)]
         for t in range(PACK):
@@ -114,9 +119,15 @@ def tile_picked_respelled_store_one_boardmixed_store_plain_kernel(
                 planes[:, t, :], xcd[t][:].indirect(half_of(offs2_sb, h)), ACT.Copy, scale=gb_sb[:, t : t + 1]
             )
 
+        def weave(woven, planes):
+            return (
+                woven.rearrange("p (c i) t -> p c t i", i=RUN),
+                planes.rearrange("p t (c i) -> p c t i", i=RUN),
+            )
+
         def quantize_slots(planes, h, woven_tag, codes_tag):
             woven = new("xc_woven%d" % h, [P, HALF, PACK], BF16, woven_tag)
-            nc.vector.tensor_copy(woven[:], planes[:].rearrange("p t j -> p j t"))
+            nc.vector.tensor_copy(*weave(woven[:], planes[:]))
             codes = new("xc_codes%d" % h, [P, HALF], U32, codes_tag)
             scales = new("xc_scales%d" % h, [P, HALF], U8)
             nc.vector.quantize_mx(codes[:].bitcast(FP8X4), scales[:], woven[:].rearrange("p j t -> p (j t)"))
@@ -161,31 +172,54 @@ def tile_picked_respelled_store_one_boardmixed_store_plain_kernel(
             read_slots(planes1, t, 1)
 
         xq0 = quantize_slots(planes0, 0, None, "turn")
-        acc_32 = first_product(xq0, 0, (3, 2))
-        acc_01 = first_product(xq0, 0, (0, 1))
-        a0 = copy_out("vector", acc_32, 0, (3, 2))
+        acc_03 = first_product(xq0, 0, (0, 3))
+        acc_12 = first_product(xq0, 0, (1, 2))
+        a0 = copy_out("vector", acc_03, 0, (0, 3))
         xq1 = quantize_slots(planes1, 1, "turn", None)
-        a0 = {**a0, **copy_out("vector", acc_01, 0, (0, 1), "turn")}
+        a0 = {**a0, **copy_out("vector", acc_12, 0, (1, 2), "turn")}
+        scatter("scalar", a0, 0, 0)
         scatter("scalar", a0, 0, 3)
-        scatter("scalar", a0, 0, 2)
-        scatter("vector", a0, 0, 0)
         scatter("vector", a0, 0, 1)
-        a1 = copy_out("scalar", first_product(xq1, 1, (3, 0)), 1, (3, 0))
-        a1 = {**a1, **copy_out("scalar", first_product(xq1, 1, (1, 2)), 1, (1, 2))}
-        scatter("scalar", a1, 1, 3)
-        for t in (0, 1, 2):
+        scatter("vector", a0, 0, 2)
+        a1 = copy_out("scalar", first_product(xq1, 1, (0, 1)), 1, (0, 1))
+        a1 = {**a1, **copy_out("scalar", first_product(xq1, 1, (2, 3)), 1, (2, 3))}
+        scatter("scalar", a1, 1, 0)
+        for t in (1, 2, 3):
             scatter("vector", a1, 1, t)
 
-        diff = new("diff", [P, PACK, O], F32)
-        for t in (3, 0, 1, 2):
-            first = new("first%d" % t, [P, O], F32)
-            nc.scalar.activation(first[:], board[t][:].indirect(offs5_sb[:]), ACT.Copy, scale=sa_sb[:, t : t + 1])
-            second = new("second%d" % t, [P, O], F32)
-            nc.scalar.activation(second[:], board[t][:].indirect(offs6_sb[:]), ACT.Copy, scale=sb_sb[:, t : t + 1])
-            nc.vector.tensor_tensor(diff[:, t, :], first[:], second[:], ALU.subtract)
+        last = PACK - 1
+        first = new("first", [P, last, O], F32)
+        second = new("second", [P, last, O], F32)
+        first_lo = new("first_lo", [P, SPLIT], F32)
+        first_hi = new("first_hi", [P, O - SPLIT], F32)
+        second_last = new("second_last", [P, O], F32)
 
+        def read_board(dst, t, offsets, weight):
+            nc.scalar.activation(dst, board[t][:].indirect(offsets), ACT.Copy, scale=weight[:, t : t + 1])
+
+        for t in range(last):
+            read_board(first[:, t, :], t, offs5_sb[:], sa_sb)
+            read_board(second[:, t, :], t, offs6_sb[:], sb_sb)
+        read_board(second_last[:], last, offs6_sb[:], sb_sb)
+        read_board(first_lo[:], last, offs5_sb[:, : SPLIT // STRIPE], sa_sb)
+        read_board(first_hi[:], last, offs5_sb[:, SPLIT // STRIPE :], sa_sb)
+
+        diff_lo = new("diff_lo", [P, PACK, SPLIT], F32)
+        diff_hi = new("diff_hi", [P, PACK, O - SPLIT], F32)
+        mag_hi = new("mag_hi", [P, PACK, O - SPLIT], BF16)
         hid = new("hid", [P, O, PACK], BF16)
-        nc.scalar.activation(hid[:], diff[:].rearrange("p t o -> p o t"), ACT.Abs)
+
+        def magnitude(dst, src):
+            nc.vector.scalar_tensor_tensor(dst, src, -1.0, src, ALU.mult, ALU.max)
+
+        nc.vector.tensor_tensor(diff_hi[:, :last, :], first[:, :, SPLIT:], second[:, :, SPLIT:], ALU.subtract)
+        nc.vector.tensor_tensor(diff_lo[:, :last, :], first[:, :, :SPLIT], second[:, :, :SPLIT], ALU.subtract)
+        magnitude(mag_hi[:, :last, :], diff_hi[:, :last, :])
+        nc.vector.tensor_tensor(diff_lo[:, last, :], first_lo[:], second_last[:, :SPLIT], ALU.subtract)
+        nc.vector.tensor_tensor(diff_hi[:, last, :], first_hi[:], second_last[:, SPLIT:], ALU.subtract)
+        nc.scalar.activation(*weave(hid[:, :SPLIT, :], diff_lo[:]), ACT.Abs)
+        magnitude(mag_hi[:, last, :], diff_hi[:, last, :])
+        nc.vector.tensor_copy(*weave(hid[:, SPLIT:, :], mag_hi[:]))
         hid_codes = new("hid_codes", [P, O], U32)
         hid_scales = new("hid_scales", [P, O], U8)
         nc.vector.quantize_mx(hid_codes[:].bitcast(FP8X4), hid_scales[:], hid[:].rearrange("p o t -> p (o t)"))

@@ -66,20 +66,23 @@ def tile_picked_respelled_store_one_boardmixed_store_plain_kernel(
         ga_sb = load_column("ga", ga, nc.scalar)
         offs_sb = load_list("offs", offs)
         nc.sync.dma_start(ta_sb[0][:], ta_rows[0])
-        gb_sb = load_column("gb", gb, nc.sync)
-        offs2_sb = load_list("offs2", offs2)
         nc.sync.dma_start(ta_sb[1][:], ta_rows[1])
-        nc.sync.dma_start(ta_sb[2][:], ta_rows[2])
+        offs2_sb = load_list("offs2", offs2)
+        gb_cols = gb.rearrange("(p t) o -> p (t o)", t=PACK)
+        gb_sb = [new("gb%d" % u, [P, 2], F32) for u in range(2)]
+        nc.sync.dma_start(gb_sb[0][:], gb_cols[:, 0:2])
         wt_plane = load_scale_rows("wt_scales", wt_scales, F)
+        vs_plane = load_scale_rows("vs_scales", vs_scales, S)
+        nc.sync.dma_start(ta_sb[2][:], ta_rows[2])
+        offs3_sb = load_list("offs3", offs3)
+        offs7_sb = load_list("offs7", offs7)
         wt_words_sb = new("wt_words", [P, 2 * F], U8)
         nc.sync.dma_start(wt_words_sb[:].bitcast(I32), wt_words[0].bitcast(I32))
-        offs3_sb = load_list("offs3", offs3)
         nc.sync.dma_start(ta_sb[3][:], ta_rows[3])
-        offs4_sb = load_list("offs4", offs4)
-        vs_plane = load_scale_rows("vs_scales", vs_scales, S)
+        nc.sync.dma_start(gb_sb[1][:], gb_cols[:, 2:4])
         vs_words_sb = new("vs_words", [P, S], I32)
         nc.sync.dma_start(vs_words_sb[:], vs_words[0].rearrange("p n t -> p (n t)").bitcast(I32))
-        offs7_sb = load_list("offs7", offs7)
+        offs4_sb = load_list("offs4", offs4)
         offs5_sb = load_list("offs5", offs5)
         offs6_sb = load_list("offs6", offs6)
         sa_sb = load_column("sa", sa, nc.sync)
@@ -116,7 +119,7 @@ def tile_picked_respelled_store_one_boardmixed_store_plain_kernel(
 
         def read_slots(planes, t, h):
             nc.scalar.activation(
-                planes[:, t, :], xcd[t][:].indirect(half_of(offs2_sb, h)), ACT.Copy, scale=gb_sb[:, t : t + 1]
+                planes[:, t, :], xcd[t][:].indirect(half_of(offs2_sb, h)), ACT.Copy, scale=gb_sb[t // 2][:, t % 2 : t % 2 + 1]
             )
 
         def weave(woven, planes):
@@ -125,9 +128,12 @@ def tile_picked_respelled_store_one_boardmixed_store_plain_kernel(
                 planes.rearrange("p t (c i) -> p c t i", i=RUN),
             )
 
-        def quantize_slots(planes, h, woven_tag, codes_tag):
-            woven = new("xc_woven%d" % h, [P, HALF, PACK], BF16, woven_tag)
+        def weave_slots(planes, h, tag):
+            woven = new("xc_woven%d" % h, [P, HALF, PACK], BF16, tag)
             nc.vector.tensor_copy(*weave(woven[:], planes[:]))
+            return woven
+
+        def quantize_slots(woven, h, codes_tag):
             codes = new("xc_codes%d" % h, [P, HALF], U32, codes_tag)
             scales = new("xc_scales%d" % h, [P, HALF], U8)
             nc.vector.quantize_mx(codes[:].bitcast(FP8X4), scales[:], woven[:].rearrange("p j t -> p (j t)"))
@@ -135,7 +141,7 @@ def tile_picked_respelled_store_one_boardmixed_store_plain_kernel(
 
         def first_product(quantized, h, pair):
             codes, scales = quantized
-            acc = psum.tile([P, 2, HALF], F32, name="acc%d%d" % (h, pair[0]))
+            acc = psum.tile([P, len(pair), HALF], F32, name="acc%d%d" % (h, pair[0]))
             for i, t in enumerate(pair):
                 nc.tensor.matmul_mx(
                     out=acc[:, i, :],
@@ -149,7 +155,7 @@ def tile_picked_respelled_store_one_boardmixed_store_plain_kernel(
             return acc
 
         def copy_out(engine, acc, h, pair, tag=None):
-            a = new("a%d%d" % (h, pair[0]), [P, 2, HALF], F32, tag)
+            a = new("a%d%d" % (h, pair[0]), [P, len(pair), HALF], F32, tag)
             if engine == "vector":
                 nc.vector.tensor_copy(a[:], acc[:])
             else:
@@ -164,26 +170,32 @@ def tile_picked_respelled_store_one_boardmixed_store_plain_kernel(
                 nc.scalar.activation(window, a[t], ACT.Copy)
 
         planes0 = new("xc_planes0", [P, PACK, HALF], BF16)
-        for t in range(PACK):
-            nc.scalar.activation(xcd[t][:], ta_sb[t][:].indirect(offs_sb[:]), ACT.Copy, scale=ga_sb[:, t : t + 1])
-            read_slots(planes0, t, 0)
+        for pair in ((0, 1), (2, 3)):
+            for t in pair:
+                nc.scalar.activation(xcd[t][:], ta_sb[t][:].indirect(offs_sb[:]), ACT.Copy, scale=ga_sb[:, t : t + 1])
+            for t in pair:
+                read_slots(planes0, t, 0)
         planes1 = new("xc_planes1", [P, PACK, HALF], BF16, "ta3")
         for t in range(PACK):
             read_slots(planes1, t, 1)
 
-        xq0 = quantize_slots(planes0, 0, None, "turn")
-        acc_03 = first_product(xq0, 0, (0, 3))
+        xq0 = quantize_slots(weave_slots(planes0, 0, None), 0, "turn")
+        acc_0 = first_product(xq0, 0, (0,))
+        acc_3 = first_product(xq0, 0, (3,))
         acc_12 = first_product(xq0, 0, (1, 2))
-        a0 = copy_out("vector", acc_03, 0, (0, 3))
-        xq1 = quantize_slots(planes1, 1, "turn", None)
-        a0 = {**a0, **copy_out("vector", acc_12, 0, (1, 2), "turn")}
+        a0 = copy_out("vector", acc_0, 0, (0,))
+        a0 = {**a0, **copy_out("vector", acc_3, 0, (3,))}
+        woven1 = weave_slots(planes1, 1, "turn")
+        a0 = {**a0, **copy_out("vector", acc_12, 0, (1, 2), "ta3")}
+        xq1 = quantize_slots(woven1, 1, None)
         scatter("scalar", a0, 0, 0)
         scatter("scalar", a0, 0, 3)
         scatter("vector", a0, 0, 1)
         scatter("vector", a0, 0, 2)
         a1 = copy_out("scalar", first_product(xq1, 1, (0, 1)), 1, (0, 1))
-        a1 = {**a1, **copy_out("scalar", first_product(xq1, 1, (2, 3)), 1, (2, 3))}
+        a1 = {**a1, **copy_out("scalar", first_product(xq1, 1, (2,)), 1, (2,))}
         scatter("scalar", a1, 1, 0)
+        a1 = {**a1, **copy_out("scalar", first_product(xq1, 1, (3,)), 1, (3,))}
         for t in (1, 2, 3):
             scatter("vector", a1, 1, t)
 
@@ -201,8 +213,8 @@ def tile_picked_respelled_store_one_boardmixed_store_plain_kernel(
             read_board(first[:, t, :], t, offs5_sb[:], sa_sb)
             read_board(second[:, t, :], t, offs6_sb[:], sb_sb)
         read_board(second_last[:], last, offs6_sb[:], sb_sb)
-        read_board(first_lo[:], last, offs5_sb[:, : SPLIT // STRIPE], sa_sb)
         read_board(first_hi[:], last, offs5_sb[:, SPLIT // STRIPE :], sa_sb)
+        read_board(first_lo[:], last, offs5_sb[:, : SPLIT // STRIPE], sa_sb)
 
         diff_lo = new("diff_lo", [P, PACK, SPLIT], F32)
         diff_hi = new("diff_hi", [P, PACK, O - SPLIT], F32)
@@ -215,8 +227,8 @@ def tile_picked_respelled_store_one_boardmixed_store_plain_kernel(
         nc.vector.tensor_tensor(diff_hi[:, :last, :], first[:, :, SPLIT:], second[:, :, SPLIT:], ALU.subtract)
         nc.vector.tensor_tensor(diff_lo[:, :last, :], first[:, :, :SPLIT], second[:, :, :SPLIT], ALU.subtract)
         magnitude(mag_hi[:, :last, :], diff_hi[:, :last, :])
-        nc.vector.tensor_tensor(diff_lo[:, last, :], first_lo[:], second_last[:, :SPLIT], ALU.subtract)
         nc.vector.tensor_tensor(diff_hi[:, last, :], first_hi[:], second_last[:, SPLIT:], ALU.subtract)
+        nc.vector.tensor_tensor(diff_lo[:, last, :], first_lo[:], second_last[:, :SPLIT], ALU.subtract)
         nc.scalar.activation(*weave(hid[:, :SPLIT, :], diff_lo[:]), ACT.Abs)
         magnitude(mag_hi[:, last, :], diff_hi[:, last, :])
         nc.vector.tensor_copy(*weave(hid[:, SPLIT:, :], mag_hi[:]))

from contextlib import ExitStack

import concourse.mybir as mybir

K, J, R, T, U, F, C, O, N, S = 512, 512, 512, 2048, 1024, 1024, 1024, 256, 256, 1024
FLOPS = 2 * K * R * J + 2 * R * N * O

F32 = mybir.dt.float32
BF16 = mybir.dt.bfloat16
I32 = mybir.dt.int32
U32 = mybir.dt.uint32
U16 = mybir.dt.uint16
U8 = mybir.dt.uint8
FP8X4 = mybir.dt.float8_e4m3fn_x4
FP4X4 = mybir.dt.float4_e2m1fn_x4
ACT = mybir.ActivationFunctionType
ALU = mybir.AluOpType

P = 128
PACK = 4
HALF = J // 2
STRIPE = 16
ALIGN = 64
RUN = 4
SPLIT = 160


def tile_picked_respelled_store_one_boardmixed_store_plain_kernel(
    tc, ta, ga, gb, wt_words, wt_scales, sa, sb, vs_words, vs_scales,
    offs, offs2, offs3, offs4, offs5, offs6, offs7, out,
):
    nc = tc.nc
    with ExitStack() as ctx:
        keep = ctx.enter_context(tc.tile_pool(name="keep", bufs=1))
        psum = ctx.enter_context(tc.psum_pool(name="psum", bufs=1))

        def new(name, shape, dtype, tag=None):
            return keep.tile(shape, dtype, name=name, tag=tag or name, align_bytes=ALIGN)

        def load_list(name, source):
            tile = new(name, list(source.shape), U16)
            nc.sync.dma_start(tile[:], source)
            return tile

        def load_column(name, source, queue):
            tile = new(name, [P, PACK], F32)
            queue.dma_start(tile[:], source.rearrange("(p t) o -> p (t o)", t=PACK))
            return tile

        def load_scale_rows(name, source, width):
            staged = new(name + "_staged", [PACK, PACK, width // 4], I32)
            nc.sync.dma_start(staged[:], source[0].bitcast(I32).rearrange("(q i) c -> i q c", i=PACK))
            plane = new(name + "_plane", [P, width], U8)
            nc.vector.memset(plane[:].bitcast(I32), 0)
            for q in range(4):
                nc.vector.tensor_copy(plane[32 * q : 32 * q + PACK, :].bitcast(I32), staged[:, q, :])
            return plane

        ta_rows = ta.rearrange("(p t) c -> t p c", t=PACK)
        ta_sb = [new("ta%d" % t, [P, T], F32) for t in range(PACK)]

        warm = new("warm", [P, 1], F32)
        nc.vector.memset(warm[:], 0.0)
        warm_out = new("warm_out", [P, 1], F32)
        nc.scalar.activation(warm_out[:], warm[:], ACT.Copy)
        ga_sb = load_column("ga", ga, nc.scalar)
        offs_sb = load_list("offs", offs)
        nc.sync.dma_start(ta_sb[0][:], ta_rows[0])
        nc.sync.dma_start(ta_sb[1][:], ta_rows[1])
        offs2_sb = load_list("offs2", offs2)
        gb_cols = gb.rearrange("(p t) o -> p (t o)", t=PACK)
        gb_sb = [new("gb%d" % u, [P, 2], F32) for u in range(2)]
        nc.sync.dma_start(gb_sb[0][:], gb_cols[:, 0:2])
        wt_plane = load_scale_rows("wt_scales", wt_scales, F)
        vs_plane = load_scale_rows("vs_scales", vs_scales, S)
        nc.sync.dma_start(ta_sb[2][:], ta_rows[2])
        offs3_sb = load_list("offs3", offs3)
        offs7_sb = load_list("offs7", offs7)
        wt_words_sb = new("wt_words", [P, 2 * F], U8)
        nc.sync.dma_start(wt_words_sb[:].bitcast(I32), wt_words[0].bitcast(I32))
        nc.sync.dma_start(ta_sb[3][:], ta_rows[3])
        nc.sync.dma_start(gb_sb[1][:], gb_cols[:, 2:4])
        vs_words_sb = new("vs_words", [P, S], I32)
        nc.sync.dma_start(vs_words_sb[:], vs_words[0].rearrange("p n t -> p (n t)").bitcast(I32))
        offs4_sb = load_list("offs4", offs4)
        offs5_sb = load_list("offs5", offs5)
        offs6_sb = load_list("offs6", offs6)
        sa_sb = load_column("sa", sa, nc.sync)
        sb_sb = load_column("sb", sb, nc.sync)

        board = [new("board%d" % t, [P, C], F32) for t in range(PACK)]
        for t in range(PACK):
            nc.vector.memset(board[t][:], 0.0)

        wt_picked_scales = new("wt_picked_scales", [P, R], U8)
        nc.vector.tensor_copy(wt_picked_scales[:], wt_plane[:].indirect(offs3_sb[:]))
        wt_picked_words = new("wt_picked_words", [P, 2 * R], U8)
        nc.vector.tensor_copy(wt_picked_words[:].bitcast(U16), wt_words_sb[:].bitcast(U16).indirect(offs3_sb[:]))
        wt_dealt_scales = new("wt_dealt_scales", [P, R], U8)
        nc.vector.tensor_copy(
            wt_dealt_scales[:].rearrange("p (t m) -> p t m", t=PACK),
            wt_picked_scales[:].rearrange("p (m t) -> p t m", t=PACK),
        )
        wt_dealt_words = new("wt_dealt_words", [P, 2 * R], U8)
        nc.vector.tensor_copy(
            wt_dealt_words[:].rearrange("p (t m b) -> p t m b", t=PACK, b=2),
            wt_picked_words[:].rearrange("p (m t b) -> p t m b", t=PACK, b=2),
        )
        vs_picked_scales = new("vs_picked_scales", [P, N], U8)
        nc.vector.tensor_copy(vs_picked_scales[:], vs_plane[:].indirect(offs7_sb[:]))
        vs_picked_words = new("vs_picked_words", [P, N], U32)
        nc.vector.tensor_copy(vs_picked_words[:], vs_words_sb[:].bitcast(U32).indirect(offs7_sb[:]))

        xcd = [new("xcd%d" % t, [P, U], F32) for t in range(PACK)]

        def half_of(offsets, h):
            cols = HALF // STRIPE
            return offsets[:, h * cols : (h + 1) * cols]

        def read_slots(planes, t, h):
            nc.scalar.activation(
                planes[:, t, :], xcd[t][:].indirect(half_of(offs2_sb, h)), ACT.Copy, scale=gb_sb[t // 2][:, t % 2 : t % 2 + 1]
            )

        def weave(woven, planes):
            return (
                woven.rearrange("p (c i) t -> p c t i", i=RUN),
                planes.rearrange("p t (c i) -> p c t i", i=RUN),
            )

        def weave_slots(planes, h, tag):
            woven = new("xc_woven%d" % h, [P, HALF, PACK], BF16, tag)
            nc.vector.tensor_copy(*weave(woven[:], planes[:]))
            return woven

        def quantize_slots(woven, h, codes_tag):
            codes = new("xc_codes%d" % h, [P, HALF], U32, codes_tag)
            scales = new("xc_scales%d" % h, [P, HALF], U8)
            nc.vector.quantize_mx(codes[:].bitcast(FP8X4), scales[:], woven[:].rearrange("p j t -> p (j t)"))
            return codes, scales

        def first_product(quantized, h, pair):
            codes, scales = quantized
            acc = psum.tile([P, len(pair), HALF], F32, name="acc%d%d" % (h, pair[0]))
            for i, t in enumerate(pair):
                nc.tensor.matmul_mx(
                    out=acc[:, i, :],
                    lhsT=wt_dealt_words[:, 2 * P * t : 2 * P * (t + 1)].bitcast(FP4X4),
                    lhsT_scale=wt_dealt_scales[:, P * t : P * (t + 1)],
                    rhs=codes[:].bitcast(FP8X4),
                    rhs_scale=scales[:],
                    start=True,
                    stop=True,
                )
            return acc

        def copy_out(engine, acc, h, pair, tag=None):
            a = new("a%d%d" % (h, pair[0]), [P, len(pair), HALF], F32, tag)
            if engine == "vector":
                nc.vector.tensor_copy(a[:], acc[:])
            else:
                nc.scalar.activation(a[:], acc[:], ACT.Copy)
            return {t: a[:, i, :] for i, t in enumerate(pair)}

        def scatter(engine, a, h, t):
            window = board[t][:].indirect(half_of(offs4_sb, h))
            if engine == "vector":
                nc.vector.tensor_copy(window, a[t])
            else:
                nc.scalar.activation(window, a[t], ACT.Copy)

        planes0 = new("xc_planes0", [P, PACK, HALF], BF16)
        for pair in ((0, 1), (2, 3)):
            for t in pair:
                nc.scalar.activation(xcd[t][:], ta_sb[t][:].indirect(offs_sb[:]), ACT.Copy, scale=ga_sb[:, t : t + 1])
            for t in pair:
                read_slots(planes0, t, 0)
        planes1 = new("xc_planes1", [P, PACK, HALF], BF16, "ta3")
        for t in range(PACK):
            read_slots(planes1, t, 1)

        xq0 = quantize_slots(weave_slots(planes0, 0, None), 0, "turn")
        acc_0 = first_product(xq0, 0, (0,))
        acc_3 = first_product(xq0, 0, (3,))
        acc_12 = first_product(xq0, 0, (1, 2))
        a0 = copy_out("vector", acc_0, 0, (0,))
        a0 = {**a0, **copy_out("vector", acc_3, 0, (3,))}
        woven1 = weave_slots(planes1, 1, "turn")
        a0 = {**a0, **copy_out("vector", acc_12, 0, (1, 2), "ta3")}
        xq1 = quantize_slots(woven1, 1, None)
        scatter("scalar", a0, 0, 0)
        scatter("scalar", a0, 0, 3)
        scatter("vector", a0, 0, 1)
        scatter("vector", a0, 0, 2)
        a1 = copy_out("scalar", first_product(xq1, 1, (0, 1)), 1, (0, 1))
        a1 = {**a1, **copy_out("scalar", first_product(xq1, 1, (2,)), 1, (2,))}
        scatter("scalar", a1, 1, 0)
        a1 = {**a1, **copy_out("scalar", first_product(xq1, 1, (3,)), 1, (3,))}
        for t in (1, 2, 3):
            scatter("vector", a1, 1, t)

        last = PACK - 1
        first = new("first", [P, last, O], F32)
        second = new("second", [P, last, O], F32)
        first_lo = new("first_lo", [P, SPLIT], F32)
        first_hi = new("first_hi", [P, O - SPLIT], F32)
        second_last = new("second_last", [P, O], F32)

        def read_board(dst, t, offsets, weight):
            nc.scalar.activation(dst, board[t][:].indirect(offsets), ACT.Copy, scale=weight[:, t : t + 1])

        for t in range(last):
            read_board(first[:, t, :], t, offs5_sb[:], sa_sb)
            read_board(second[:, t, :], t, offs6_sb[:], sb_sb)
        read_board(second_last[:], last, offs6_sb[:], sb_sb)
        read_board(first_hi[:], last, offs5_sb[:, SPLIT // STRIPE :], sa_sb)
        read_board(first_lo[:], last, offs5_sb[:, : SPLIT // STRIPE], sa_sb)

        diff_lo = new("diff_lo", [P, PACK, SPLIT], F32)
        diff_hi = new("diff_hi", [P, PACK, O - SPLIT], F32)
        mag_hi = new("mag_hi", [P, PACK, O - SPLIT], BF16)
        hid = new("hid", [P, O, PACK], BF16)

        def magnitude(dst, src):
            nc.vector.scalar_tensor_tensor(dst, src, -1.0, src, ALU.mult, ALU.max)

        nc.vector.tensor_tensor(diff_hi[:, :last, :], first[:, :, SPLIT:], second[:, :, SPLIT:], ALU.subtract)
        nc.vector.tensor_tensor(diff_lo[:, :last, :], first[:, :, :SPLIT], second[:, :, :SPLIT], ALU.subtract)
        magnitude(mag_hi[:, :last, :], diff_hi[:, :last, :])
        nc.vector.tensor_tensor(diff_hi[:, last, :], first_hi[:], second_last[:, SPLIT:], ALU.subtract)
        nc.vector.tensor_tensor(diff_lo[:, last, :], first_lo[:], second_last[:, :SPLIT], ALU.subtract)
        nc.scalar.activation(*weave(hid[:, :SPLIT, :], diff_lo[:]), ACT.Abs)
        magnitude(mag_hi[:, last, :], diff_hi[:, last, :])
        nc.vector.tensor_copy(*weave(hid[:, SPLIT:, :], mag_hi[:]))
        hid_codes = new("hid_codes", [P, O], U32)
        hid_scales = new("hid_scales", [P, O], U8)
        nc.vector.quantize_mx(hid_codes[:].bitcast(FP8X4), hid_scales[:], hid[:].rearrange("p o t -> p (o t)"))

        for i in range(N // P):
            y = psum.tile([P, O], F32, name="y%d" % i)
            nc.tensor.matmul_mx(
                out=y[:],
                lhsT=vs_picked_words[:, P * i : P * (i + 1)].bitcast(FP8X4),
                lhsT_scale=vs_picked_scales[:, P * i : P * (i + 1)],
                rhs=hid_codes[:].bitcast(FP8X4),
                rhs_scale=hid_scales[:],
                start=True,
                stop=True,
            )
            y_sb = new("y_sb%d" % i, [P, O], F32)
            if i == 0:
                nc.vector.tensor_copy(y_sb[:], y[:])
                nc.sync.dma_start(out[P * i : P * (i + 1), :], y_sb[:])
            else:
                nc.scalar.activation(y_sb[:], y[:], ACT.Copy)
                nc.scalar.dma_start(out[P * i : P * (i + 1), :], y_sb[:])
